import numpy as np
CORES = [68,69,70,71,76,77,78,79,84,85,86,87,92,93,94,95]
N = 16
ROOT = 6
def setup_inputs(rng):
    return {"x": rng.standard_normal((N, 128, 128), dtype=np.float32)}
def reference(x):
    return {"y": np.broadcast_to(x[ROOT], x.shape)}

@@ -1,0 +1,72 @@
+from concourse.bass import DstId, RemoteDMATransfer
+
+Q = 4
+
+SCRATCH = {
+    "d": ("dram", [Q, 128, 32], "float32"),
+}
+SEMAPHORES = ["loaded", "own", "peer", "sent", "stored"]
+
+
+def rank_program(g, core, T, topo):
+    rank = T.rank_of(core)
+    if rank is None:
+        return
+    sem = T.sem
+    root = T.cores[T.root]
+
+    def dst(c):
+        rid, pid, se = topo.addr(c)
+        return DstId(rid=rid, pnc=pid)
+
+    on_chip = {}
+    for c in T.cores:
+        on_chip.setdefault(topo.chip(c), []).append(c)
+    rchip = topo.chip(root)
+
+    def distance(ch):
+        if topo.mates(rchip, ch):
+            return 0
+        return 1 if topo.same_plane(rchip, ch) else 2
+
+    far_chips = sorted((ch for ch in on_chip if ch != rchip), key=distance, reverse=True)
+
+    if core == root:
+        g.sync.dma_start(T.d[:], T.x[:]).then_inc(sem.loaded, 16)
+        g.wait_ge(sem.loaded, 16)
+        g.remote_dma_fused(
+            [RemoteDMATransfer(dst_ids=[dst(on_chip[ch][q]) for ch in far_chips],
+                               dma_engine_mask=0x3 << (2 * q), remote_sem=sem.own,
+                               srcs=[T.d[q]], dsts=[T.d[q] for ch in far_chips])
+             for q in range(Q)],
+            local_sem=sem.sent)
+        near = [c for c in on_chip[rchip] if c != root]
+        g.remote_dma_fused(
+            [RemoteDMATransfer(dst_ids=[dst(c) for c in near],
+                               dma_engine_mask=0x300 << (2 * q), remote_sem=sem.peer,
+                               srcs=[T.d[q]], dsts=[T.d[q] for c in near])
+             for q in range(Q)],
+            local_sem=sem.sent)
+        g.sync.wait_ge(sem.sent, 4 * Q)
+        g.sync.dma_start(T.y[:], T.x[:]).then_inc(sem.stored, 16)
+        g.sync.wait_ge(sem.stored, 16)
+        return
+
+    mine = on_chip[topo.chip(core)]
+    if topo.chip(core) == rchip:
+        g.sync.wait_ge(sem.peer, 2 * Q)
+    else:
+        q = mine.index(core)
+        peers = [c for c in mine if c != core]
+        g.wait_ge(sem.own, 2)
+        g.remote_dma_fused(
+            [RemoteDMATransfer(dst_ids=[dst(c)], dma_engine_mask=0xF << (4 * i), remote_sem=sem.peer,
+                               srcs=[T.d[q]], dsts=[T.d[q]])
+             for i, c in enumerate(peers)],
+            local_sem=sem.sent)
+        g.sync.wait_ge(sem.own, 2)
+        g.sync.wait_ge(sem.peer, 4 * len(peers))
+    g.sync.dma_start(T.y[:], T.d[:]).then_inc(sem.stored, 16)
+    g.sync.wait_ge(sem.stored, 16)
+    if topo.chip(core) != rchip:
+        g.wait_ge(sem.sent, 4 * (len(mine) - 1))

@@ -1,11 +1,14 @@
 from concourse.bass import DstId, RemoteDMATransfer
 
 Q = 4
+BR = 24
+AR = 128 - BR
 
 SCRATCH = {
-    "d": ("dram", [Q, 128, 32], "float32"),
+    "dA": ("dram", [Q, 128, AR // Q], "float32"),
+    "dB": ("dram", [128, BR], "float32"),
 }
-SEMAPHORES = ["loaded", "own", "peer", "sent", "stored"]
+SEMAPHORES = ["loadA", "loadB", "own", "peer", "direct", "sent", "storeA", "storeB"]
 
 
 def rank_program(g, core, T, topo):
@@ -32,41 +35,55 @@ def rank_program(g, core, T, topo):
     far_chips = sorted((ch for ch in on_chip if ch != rchip), key=distance, reverse=True)
 
     if core == root:
-        g.sync.dma_start(T.d[:], T.x[:]).then_inc(sem.loaded, 16)
-        g.wait_ge(sem.loaded, 16)
+        near = [c for c in on_chip[rchip] if c != root]
+        g.sync.dma_start(T.dA[:], T.x[0:AR, :]).then_inc(sem.loadA, 16)
+        g.scalar.dma_start(T.dB[:], T.x[AR:128, :]).then_inc(sem.loadB, 16)
+        g.wait_ge(sem.loadA, 16)
         g.remote_dma_fused(
             [RemoteDMATransfer(dst_ids=[dst(on_chip[ch][q]) for ch in far_chips],
                                dma_engine_mask=0x3 << (2 * q), remote_sem=sem.own,
-                               srcs=[T.d[q]], dsts=[T.d[q] for ch in far_chips])
-             for q in range(Q)],
-            local_sem=sem.sent)
-        near = [c for c in on_chip[rchip] if c != root]
-        g.remote_dma_fused(
+                               srcs=[T.dA[q]], dsts=[T.dA[q] for ch in far_chips])
+             for q in range(Q)] +
             [RemoteDMATransfer(dst_ids=[dst(c) for c in near],
                                dma_engine_mask=0x300 << (2 * q), remote_sem=sem.peer,
-                               srcs=[T.d[q]], dsts=[T.d[q] for c in near])
+                               srcs=[T.dA[q]], dsts=[T.dA[q] for c in near])
              for q in range(Q)],
             local_sem=sem.sent)
-        g.sync.wait_ge(sem.sent, 4 * Q)
-        g.sync.dma_start(T.y[:], T.x[:]).then_inc(sem.stored, 16)
-        g.sync.wait_ge(sem.stored, 16)
+        g.wait_ge(sem.loadB, 16)
+        g.remote_dma_fused(
+            [RemoteDMATransfer(dst_ids=[dst(on_chip[ch][j]) for ch in far_chips],
+                               dma_engine_mask=0x3 << (2 * j), remote_sem=sem.direct,
+                               srcs=[T.dB[:]], dsts=[T.dB[:] for ch in far_chips])
+             for j in range(Q)] +
+            [RemoteDMATransfer(dst_ids=[dst(c) for c in near],
+                               dma_engine_mask=0xFF00, remote_sem=sem.direct,
+                               srcs=[T.dB[:]], dsts=[T.dB[:] for c in near])],
+            local_sem=sem.sent)
+        g.sync.wait_ge(sem.sent, 32)
+        g.sync.dma_start(T.y[:], T.x[:]).then_inc(sem.storeA, 16)
+        g.sync.wait_ge(sem.storeA, 16)
         return
 
     mine = on_chip[topo.chip(core)]
-    if topo.chip(core) == rchip:
+    is_near = topo.chip(core) == rchip
+    if is_near:
         g.sync.wait_ge(sem.peer, 2 * Q)
+        g.scalar.wait_ge(sem.direct, 8)
     else:
         q = mine.index(core)
         peers = [c for c in mine if c != core]
         g.wait_ge(sem.own, 2)
         g.remote_dma_fused(
             [RemoteDMATransfer(dst_ids=[dst(c)], dma_engine_mask=0xF << (4 * i), remote_sem=sem.peer,
-                               srcs=[T.d[q]], dsts=[T.d[q]])
+                               srcs=[T.dA[q]], dsts=[T.dA[q]])
              for i, c in enumerate(peers)],
             local_sem=sem.sent)
         g.sync.wait_ge(sem.own, 2)
         g.sync.wait_ge(sem.peer, 4 * len(peers))
-    g.sync.dma_start(T.y[:], T.d[:]).then_inc(sem.stored, 16)
-    g.sync.wait_ge(sem.stored, 16)
-    if topo.chip(core) != rchip:
+        g.scalar.wait_ge(sem.direct, 2)
+    g.sync.dma_start(T.y[0:AR, :], T.dA[:]).then_inc(sem.storeA, 16)
+    g.scalar.dma_start(T.y[AR:128, :], T.dB[:]).then_inc(sem.storeB, 16)
+    g.sync.wait_ge(sem.storeA, 16)
+    g.scalar.wait_ge(sem.storeB, 16)
+    if not is_near:
         g.wait_ge(sem.sent, 4 * (len(mine) - 1))

from concourse.bass import DstId, RemoteDMATransfer

Q = 4
BR = 24
AR = 128 - BR

SCRATCH = {
    "dA": ("dram", [Q, 128, AR // Q], "float32"),
    "dB": ("dram", [128, BR], "float32"),
}
SEMAPHORES = ["loadA", "loadB", "own", "peer", "direct", "sent", "storeA", "storeB"]


def rank_program(g, core, T, topo):
    rank = T.rank_of(core)
    if rank is None:
        return
    sem = T.sem
    root = T.cores[T.root]

    def dst(c):
        rid, pid, se = topo.addr(c)
        return DstId(rid=rid, pnc=pid)

    on_chip = {}
    for c in T.cores:
        on_chip.setdefault(topo.chip(c), []).append(c)
    rchip = topo.chip(root)

    def distance(ch):
        if topo.mates(rchip, ch):
            return 0
        return 1 if topo.same_plane(rchip, ch) else 2

    far_chips = sorted((ch for ch in on_chip if ch != rchip), key=distance, reverse=True)

    if core == root:
        near = [c for c in on_chip[rchip] if c != root]
        g.sync.dma_start(T.dA[:], T.x[0:AR, :]).then_inc(sem.loadA, 16)
        g.scalar.dma_start(T.dB[:], T.x[AR:128, :]).then_inc(sem.loadB, 16)
        g.wait_ge(sem.loadA, 16)
        g.remote_dma_fused(
            [RemoteDMATransfer(dst_ids=[dst(on_chip[ch][q]) for ch in far_chips],
                               dma_engine_mask=0x3 << (2 * q), remote_sem=sem.own,
                               srcs=[T.dA[q]], dsts=[T.dA[q] for ch in far_chips])
             for q in range(Q)] +
            [RemoteDMATransfer(dst_ids=[dst(c) for c in near],
                               dma_engine_mask=0x300 << (2 * q), remote_sem=sem.peer,
                               srcs=[T.dA[q]], dsts=[T.dA[q] for c in near])
             for q in range(Q)],
            local_sem=sem.sent)
        g.wait_ge(sem.loadB, 16)
        g.remote_dma_fused(
            [RemoteDMATransfer(dst_ids=[dst(on_chip[ch][j]) for ch in far_chips],
                               dma_engine_mask=0x3 << (2 * j), remote_sem=sem.direct,
                               srcs=[T.dB[:]], dsts=[T.dB[:] for ch in far_chips])
             for j in range(Q)] +
            [RemoteDMATransfer(dst_ids=[dst(c) for c in near],
                               dma_engine_mask=0xFF00, remote_sem=sem.direct,
                               srcs=[T.dB[:]], dsts=[T.dB[:] for c in near])],
            local_sem=sem.sent)
        g.sync.wait_ge(sem.sent, 32)
        g.sync.dma_start(T.y[:], T.x[:]).then_inc(sem.storeA, 16)
        g.sync.wait_ge(sem.storeA, 16)
        return

    mine = on_chip[topo.chip(core)]
    is_near = topo.chip(core) == rchip
    if is_near:
        g.sync.wait_ge(sem.peer, 2 * Q)
        g.scalar.wait_ge(sem.direct, 8)
    else:
        q = mine.index(core)
        peers = [c for c in mine if c != core]
        g.wait_ge(sem.own, 2)
        g.remote_dma_fused(
            [RemoteDMATransfer(dst_ids=[dst(c)], dma_engine_mask=0xF << (4 * i), remote_sem=sem.peer,
                               srcs=[T.dA[q]], dsts=[T.dA[q]])
             for i, c in enumerate(peers)],
            local_sem=sem.sent)
        g.sync.wait_ge(sem.own, 2)
        g.sync.wait_ge(sem.peer, 4 * len(peers))
        g.scalar.wait_ge(sem.direct, 2)
    g.sync.dma_start(T.y[0:AR, :], T.dA[:]).then_inc(sem.storeA, 16)
    g.scalar.dma_start(T.y[AR:128, :], T.dB[:]).then_inc(sem.storeB, 16)
    g.sync.wait_ge(sem.storeA, 16)
    g.scalar.wait_ge(sem.storeB, 16)
    if not is_near:
        g.wait_ge(sem.sent, 4 * (len(mine) - 1))
